import numpy as np
import ml_dtypes


def mxq(x, axis, fmt="e4m3"):
    dtype, down = {"e4m3": (ml_dtypes.float8_e4m3fn, 7), "e5m2": (ml_dtypes.float8_e5m2, 14)}[fmt]
    v = np.moveaxis(np.asarray(x, np.float32).astype(ml_dtypes.bfloat16).astype(np.float64), axis, -1)
    blocks = v.reshape(v.shape[:-1] + (-1, 32))
    amax = np.abs(blocks).max(-1, keepdims=True)
    byte = np.maximum(np.where(amax > 0, np.frexp(amax)[1] - 1 + 127, 0) - down, 1)
    scale = np.exp2(byte - 127.0)
    codes = (blocks / scale).astype(np.float32).astype(dtype).astype(np.float64)
    return np.moveaxis((codes * scale).reshape(v.shape), -1, axis)


WIDE = False


def mx_kscale(k):
    if not WIDE:
        return np.ones(k)
    levels = np.array([10, -10, 5, -5, 0])
    if k % 512:
        return np.exp2(np.random.permutation(np.resize(levels, k // 32))).repeat(32)
    a = np.empty((k // 512, 16))
    for p in range(k // 512):
        a[p, :8] = np.random.permutation(np.resize(levels, 8))
        for g in range(8):
            far = levels[np.abs(levels - a[p, g]) >= 10]
            a[p, g + 8] = far[np.random.randint(len(far))]
    return np.exp2(a.ravel()).repeat(32)


def f64(x):
    return np.asarray(x).astype(np.float64)


def striped8(idx):
    return np.concatenate([x.reshape(-1, 16).T for x in idx]).astype(np.uint16)


def runs(offs, k):
    lists = np.stack([offs[16 * r : 16 * r + 16].T.reshape(-1) for r in range(8)]).astype(np.int64)
    return lists[np.arange(k) % 512 // 64]


def pack_weight(w):
    k, n = w.shape
    w = f64(np.asarray(w, np.float32).astype(ml_dtypes.bfloat16)).reshape(k // 32, 32, n)
    amax = np.abs(w).max(1)
    byte = np.clip(np.where(amax > 0, np.frexp(amax)[1] - 1 + 127 - 7, 1), 1, 254)
    scaled = (w * np.exp2(127.0 - byte)[:, None, :]).reshape(k, n).astype(np.float32)
    words = np.ascontiguousarray(scaled.reshape(k // 512, 128, 4, n).transpose(0, 1, 3, 2)).astype(ml_dtypes.float8_e4m3fn).view(np.uint8)
    return words, np.ascontiguousarray(byte.astype(np.uint8).reshape(k // 512, 16, n))


def unpack_weight(words, scales):
    g, p, n, _ = words.shape
    vals = np.ascontiguousarray(words).view(ml_dtypes.float8_e4m3fn).astype(np.float64) * np.repeat(np.exp2(scales.astype(np.float64) - 127.0), 8, axis=1)[..., None]
    return vals.transpose(0, 1, 3, 2).reshape(g * 512, n)


def sigmoid(v):
    return 1.0 / (1.0 + np.exp(-np.maximum(v, -700.0)))


K, T, S, N, H, U = 512, 2048, 512, 512, 512, 1024


def setup_inputs():
    n = np.random.standard_normal
    s = mx_kscale(K)[:, None]
    u = mx_kscale(H)
    packed_xT = pack_weight(n((K, T)) * s)
    return {
        "x_words": packed_xT[0],
        "x_scales": packed_xT[1],
        "w1": (n((K, H)) / np.sqrt(K) / s).astype(np.float32),
        "gn": (np.random.uniform(0.5, 1.5, (H, 1)) * u[:, None]).astype(np.float32),
        "w2": (n((H, N)) / np.sqrt(H) / u[:, None]).astype(np.float32),
        "mem": n((N, U)).astype(np.float32),
        "offs": striped8(np.random.randint(0, T, (8, S))),
        "n1": striped8(np.stack([np.random.permutation(S) for _ in range(8)])),
        "n2": striped8(np.stack([np.random.permutation(S) for _ in range(8)])),
        "n3": striped8(np.stack([np.random.permutation(U)[:S] for _ in range(8)])),
    }


def reference(x_words, x_scales, w1, gn, w2, mem, offs, n1, n2, n3):
    old = f64(mem)[np.arange(N)[:, None], runs(n3, N)]
    xq = unpack_weight(x_words, x_scales)[np.arange(K)[:, None], runs(offs, K)]
    y = mxq(f64(w1), 0, "e4m3").T @ xq
    z = f64(gn) * (y - (np.minimum(y[np.arange(H)[:, None], runs(n1, H)], y[np.arange(H)[:, None], runs(n2, H)])))
    h = mxq(f64(w2), 0, "e4m3").T @ mxq(z, 0, "e4m3")
    nw = old + sigmoid(h) * (h - old)
    out = f64(mem).copy()
    out[np.arange(N)[:, None], runs(n3, N)] = nw
    return out

@@ -1,0 +1,223 @@
+from contextlib import ExitStack
+
+import concourse.mybir as mybir
+
+K, T, S, N, H, U = 512, 2048, 512, 512, 512, 1024
+FLOPS = 2 * K * H * S + 2 * H * N * S
+
+F32 = mybir.dt.float32
+BF16 = mybir.dt.bfloat16
+I32 = mybir.dt.int32
+U32 = mybir.dt.uint32
+U16 = mybir.dt.uint16
+U8 = mybir.dt.uint8
+FP8X4 = mybir.dt.float8_e4m3fn_x4
+ALU = mybir.AluOpType
+ACT = mybir.ActivationFunctionType
+
+P = 128
+PACK = 4
+GROUP = 16
+CHUNK = 256
+HALVES = 2
+
+
+def tile_picked_hashunderpaget_none_p_kernel(
+    tc, x_words, x_scales, w1, gn, w2, mem, offs, n1, n2, n3, out
+):
+    nc = tc.nc
+    with ExitStack() as ctx:
+        lists = ctx.enter_context(tc.tile_pool(name="lists", bufs=1))
+        keep = ctx.enter_context(tc.tile_pool(name="keep", bufs=1))
+        psum = ctx.enter_context(tc.psum_pool(name="psum", bufs=1))
+
+        def load_list(src, name):
+            tile = lists.tile([P, S // GROUP], U16, name=name)
+            nc.sync.dma_start(tile[:], src)
+            return tile
+
+        def entries(tile, c):
+            return tile[:, c * CHUNK // GROUP : (c + 1) * CHUNK // GROUP]
+
+        offs_sb = load_list(offs, "offs_sb")
+        scale_table = keep.tile([P, T], U8, name="scale_table", tag="scales_gain")
+        nc.sync.dma_start(
+            scale_table[:].bitcast(I32), x_scales[0].bitcast(I32).unsqueeze(1).to_broadcast([16, 8, T // 4])
+        )
+        n1_sb = load_list(n1, "n1_sb")
+        n2_sb = load_list(n2, "n2_sb")
+        n3_sb = load_list(n3, "n3_sb")
+
+        word_table = keep.tile([P, T], U32, name="word_table", tag="words_w2")
+        nc.sync.dma_start(word_table[:].bitcast(I32), x_words[0].rearrange("p n t -> p (n t)").bitcast(I32))
+
+        w1_rows = w1.rearrange("(p j) c -> p j c", j=PACK)
+        half = H // HALVES
+        w1_raw = []
+        for u in range(HALVES):
+            raw = keep.tile([P, PACK, half], F32, name=f"w1_raw{u}", tag=f"stage{u}", align_bytes=64)
+            nc.sync.dma_start(raw[:], w1_rows[:, :, u * half : (u + 1) * half])
+            w1_raw.append(raw)
+
+        picked_bytes = keep.tile([P, S], U8, name="picked_bytes", tag="stage2", align_bytes=64)
+        nc.vector.tensor_copy(picked_bytes[:], scale_table[:].indirect(offs_sb[:]))
+        x_plane = keep.tile([P, S], U8, name="x_plane", align_bytes=64)
+        nc.vector.memset(x_plane[:].bitcast(I32), 0)
+        for i in range(4):
+            nc.scalar.dma_start(
+                x_plane[:].bitcast(I32)[i:P:32, :], picked_bytes[:].bitcast(I32)[8 * i : P : 32, :]
+            )
+        gain = keep.tile([P, PACK], F32, name="gain", tag="scales_gain")
+        nc.sync.dma_start(gain[:], gn.rearrange("(p t) o -> p (t o)", t=PACK))
+        x_codes = keep.tile([P, S], U32, name="x_codes", align_bytes=64)
+        nc.vector.tensor_copy(x_codes[:], word_table[:].indirect(offs_sb[:]))
+
+        def deal_columns(grouped, raw, m0):
+            ms = raw.shape[2] // PACK
+            nc.vector.tensor_copy(
+                grouped[:, :, m0 : m0 + ms, :].rearrange("p t m j -> p m j t"),
+                raw[:].rearrange("p j (m t) -> p m j t", t=PACK),
+            )
+
+        w1_grouped = keep.tile([P, PACK, P, PACK], BF16, name="w1_grouped", tag="stage3", align_bytes=64)
+        for u in range(HALVES):
+            deal_columns(w1_grouped, w1_raw[u], u * P // HALVES)
+        w1_codes = keep.tile([P, H], U32, name="w1_codes", align_bytes=64)
+        w1_plane = keep.tile([P, H], U8, name="w1_plane", align_bytes=64)
+        y = []
+        for t in range(PACK):
+            cols = slice(t * P, (t + 1) * P)
+            nc.vector.quantize_mx(
+                out=w1_codes[:, cols].bitcast(FP8X4),
+                scales=w1_plane[:, cols],
+                in_=w1_grouped[:, t].rearrange("p m j -> p (m j)"),
+            )
+        for t in range(PACK):
+            cols = slice(t * P, (t + 1) * P)
+            bank = psum.tile([P, S], F32, name=f"y_bank{t}", tag=f"bank{t}")
+            nc.tensor.matmul_mx(
+                out=bank[:],
+                lhsT=w1_codes[:, cols].bitcast(FP8X4),
+                lhsT_scale=w1_plane[:, cols],
+                rhs=x_codes[:].bitcast(FP8X4),
+                rhs_scale=x_plane[:],
+                start=True,
+                stop=True,
+            )
+            y_t = keep.tile([P, S], F32, name=f"y{t}")
+            if t == 0:
+                nc.scalar.copy(y_t[:], bank[:])
+            else:
+                nc.vector.tensor_copy(y_t[:], bank[:])
+            y.append(y_t)
+
+        w2_raw = keep.tile([P, PACK, N], F32, name="w2_raw", tag="words_w2")
+        nc.sync.dma_start(w2_raw[:], w2.rearrange("(p j) c -> p j c", j=PACK))
+        mem_rows = mem.rearrange("(b t r) u -> t b r u", t=PACK, r=8)
+        out_rows = out.rearrange("(b t r) u -> t b r u", t=PACK, r=8)
+        page = []
+        for t in range(PACK):
+            tile = keep.tile([P, U], F32, name=f"page{t}", tag=f"stage{t}", align_bytes=64)
+            nc.sync.dma_start(tile[:], mem_rows[t])
+            page.append(tile)
+
+        diff = [keep.tile([P, PACK, CHUNK], F32, name=f"diff{c}") for c in range(2)]
+
+        def fetch_pair(c, t):
+            if c == 1 and t == 0:
+                both = keep.tile([P, 2, CHUNK], F32, name="pair1_0", tag="z0", align_bytes=64)
+                a, b = both[:, 0, :], both[:, 1, :]
+            elif c == 1:
+                a = keep.tile([P, CHUNK], F32, name=f"a{c}_{t}", tag=f"th0_{t - 1}")[:]
+                b = keep.tile([P, CHUNK], F32, name=f"b{c}_{t}", tag=f"old_half0_{t - 1}")[:]
+            else:
+                a = keep.tile([P, CHUNK], F32, name=f"a{c}_{t}", tag=f"a0_{t}", align_bytes=64)[:]
+                b = keep.tile([P, CHUNK], F32, name=f"b{c}_{t}")[:]
+            nc.scalar.activation(a, y[t][:].indirect(entries(n1_sb, c)), ACT.Copy)
+            nc.scalar.activation(b, y[t][:].indirect(entries(n2_sb, c)), ACT.Copy)
+            return a, b
+
+        def less_smaller(c, t, a, b):
+            low = keep.tile([P, CHUNK], F32, name=f"low{c}_{t}", tag=f"low{c}_{t}")
+            nc.vector.tensor_tensor(low[:], a, b, ALU.min)
+            nc.vector.tensor_tensor(diff[c][:, t, :], y[t][:, c * CHUNK : (c + 1) * CHUNK], low[:], ALU.subtract)
+
+        def quantise_z(c):
+            z = keep.tile([P, CHUNK, PACK], BF16, name=f"z{c}", tag=f"z{c}", align_bytes=64)
+            nc.vector.tensor_tensor(
+                z[:].rearrange("p (c i) t -> p c t i", i=4),
+                diff[c][:].rearrange("p t (c i) -> p c t i", i=4),
+                gain[:].unsqueeze(1).unsqueeze(3).to_broadcast([P, CHUNK // 4, PACK, 4]),
+                ALU.mult,
+            )
+            z_codes = keep.tile([P, CHUNK], U32, name=f"z_codes{c}", align_bytes=64)
+            z_plane = keep.tile([P, CHUNK], U8, name=f"z_plane{c}", align_bytes=64)
+            nc.vector.quantize_mx(
+                out=z_codes[:].bitcast(FP8X4), scales=z_plane[:], in_=z[:].rearrange("p n t -> p (n t)")
+            )
+            return z_codes, z_plane
+
+        def quantise_w2(t):
+            grouped = keep.tile([P, P, PACK], BF16, name=f"w2_grouped{t}", tag=f"a0_{t}" if t else "w2_first", align_bytes=64)
+            codes = keep.tile([P, P], U32, name=f"w2_codes{t}", align_bytes=64)
+            plane = keep.tile([P, P], U8, name=f"w2_plane{t}", align_bytes=64)
+            copy = nc.vector.tensor_copy if t == 0 else nc.scalar.copy
+            copy(
+                grouped[:].rearrange("p (b s i) j -> p b s j i", s=2, i=4),
+                w2_raw[:].rearrange("p j (b t s i) -> p t b s j i", t=PACK, s=2, i=4)[:, t],
+            )
+            nc.vector.quantize_mx(
+                out=codes[:].bitcast(FP8X4), scales=plane[:], in_=grouped[:].rearrange("p m j -> p (m j)")
+            )
+            return codes, plane
+
+        def fetch_old(c, t):
+            old_half = keep.tile([P, CHUNK], F32, name=f"old_half{c}_{t}", tag=f"old_half0_{t}" if c == 0 else ["th0_2", "old_half0_2", "low1_3", "th0_3"][t])
+            nc.scalar.activation(old_half[:], page[t][:].indirect(entries(n3_sb, c)), ACT.Copy, scale=0.5)
+            return old_half
+
+        def gate(c, t, w2_q, z_q):
+            bank = psum.tile([P, CHUNK], F32, name=f"h_bank{c}_{t}", tag=f"bank{(PACK * (c + 1) + t) % 8}")
+            nc.tensor.matmul_mx(
+                out=bank[:],
+                lhsT=w2_q[0][:].bitcast(FP8X4),
+                lhsT_scale=w2_q[1][:],
+                rhs=z_q[0][:].bitcast(FP8X4),
+                rhs_scale=z_q[1][:],
+                start=True,
+                stop=True,
+            )
+            th = keep.tile([P, CHUNK], F32, name=f"th{c}_{t}", tag=f"th{c}_{t}")
+            gated = keep.tile([P, CHUNK], F32, name=f"gated{c}_{t}")
+            nc.scalar.activation(gated[:], bank[:], ACT.Silu)
+            nc.scalar.activation(th[:], bank[:], ACT.Tanh, scale=-0.5)
+            return th, gated
+
+        def write_page(c, t, old_half, th, gated):
+            kept = keep.tile([P, CHUNK], F32, name=f"kept{c}_{t}")
+            nc.vector.scalar_tensor_tensor(kept[:], th[:], 1.0, old_half[:], ALU.add, ALU.mult)
+            nc.vector.tensor_tensor(page[t][:].indirect(entries(n3_sb, c)), kept[:], gated[:], ALU.add)
+
+        w2_q = []
+        for t in range(PACK):
+            less_smaller(0, t, *fetch_pair(0, t))
+            if t == 1:
+                w2_q.append(quantise_w2(0))
+        z_first = quantise_z(0)
+        for t in range(1, PACK):
+            w2_q.append(quantise_w2(t))
+
+        olds = {}
+        gates = {}
+        for t in range(PACK):
+            olds[t] = fetch_old(0, t)
+            gates[t] = gate(0, t, w2_q[t], z_first)
+            pair = fetch_pair(1, t)
+            if t < PACK - 1:
+                write_page(0, t, olds[t], *gates[t])
+            less_smaller(1, t, *pair)
+        z_second = quantise_z(1)
+        write_page(0, PACK - 1, olds[PACK - 1], *gates[PACK - 1])
+        for t in range(PACK):
+            write_page(1, t, fetch_old(1, t), *gate(1, t, w2_q[t], z_second))
+            nc.sync.dma_start(out_rows[t], page[t][:])

@@ -39,27 +39,25 @@ def tile_picked_hashunderpaget_none_p_kernel(
         def entries(tile, c):
             return tile[:, c * CHUNK // GROUP : (c + 1) * CHUNK // GROUP]
 
+        warm_in = keep.tile([P, 1], F32, name="warm_in")
+        warm_out = keep.tile([P, 1], F32, name="warm_out")
+        nc.vector.memset(warm_in[:], 0.0)
+        nc.scalar.activation(warm_out[:], warm_in[:], ACT.Silu)
+
         offs_sb = load_list(offs, "offs_sb")
         scale_table = keep.tile([P, T], U8, name="scale_table", tag="scales_gain")
         nc.sync.dma_start(
             scale_table[:].bitcast(I32), x_scales[0].bitcast(I32).unsqueeze(1).to_broadcast([16, 8, T // 4])
         )
         n1_sb = load_list(n1, "n1_sb")
+        w1_raw = keep.tile([P, PACK, H], F32, name="w1_raw", tag="weights")
+        nc.sync.dma_start(w1_raw[:], w1.rearrange("(p j) c -> p j c", j=PACK))
+        word_table = keep.tile([P, T], U32, name="word_table", tag="page2", align_bytes=64)
+        nc.sync.dma_start(word_table[:].bitcast(I32), x_words[0].rearrange("p n t -> p (n t)").bitcast(I32))
         n2_sb = load_list(n2, "n2_sb")
         n3_sb = load_list(n3, "n3_sb")
 
-        word_table = keep.tile([P, T], U32, name="word_table", tag="words_w2")
-        nc.sync.dma_start(word_table[:].bitcast(I32), x_words[0].rearrange("p n t -> p (n t)").bitcast(I32))
-
-        w1_rows = w1.rearrange("(p j) c -> p j c", j=PACK)
-        half = H // HALVES
-        w1_raw = []
-        for u in range(HALVES):
-            raw = keep.tile([P, PACK, half], F32, name=f"w1_raw{u}", tag=f"stage{u}", align_bytes=64)
-            nc.sync.dma_start(raw[:], w1_rows[:, :, u * half : (u + 1) * half])
-            w1_raw.append(raw)
-
-        picked_bytes = keep.tile([P, S], U8, name="picked_bytes", tag="stage2", align_bytes=64)
+        picked_bytes = keep.tile([P, S], U8, name="picked_bytes", tag="page1", align_bytes=64)
         nc.vector.tensor_copy(picked_bytes[:], scale_table[:].indirect(offs_sb[:]))
         x_plane = keep.tile([P, S], U8, name="x_plane", align_bytes=64)
         nc.vector.memset(x_plane[:].bitcast(I32), 0)
@@ -69,81 +67,75 @@ def tile_picked_hashunderpaget_none_p_kernel(
             )
         gain = keep.tile([P, PACK], F32, name="gain", tag="scales_gain")
         nc.sync.dma_start(gain[:], gn.rearrange("(p t) o -> p (t o)", t=PACK))
-        x_codes = keep.tile([P, S], U32, name="x_codes", align_bytes=64)
-        nc.vector.tensor_copy(x_codes[:], word_table[:].indirect(offs_sb[:]))
 
-        def deal_columns(grouped, raw, m0):
-            ms = raw.shape[2] // PACK
-            nc.vector.tensor_copy(
-                grouped[:, :, m0 : m0 + ms, :].rearrange("p t m j -> p m j t"),
-                raw[:].rearrange("p j (m t) -> p m j t", t=PACK),
-            )
-
-        w1_grouped = keep.tile([P, PACK, P, PACK], BF16, name="w1_grouped", tag="stage3", align_bytes=64)
-        for u in range(HALVES):
-            deal_columns(w1_grouped, w1_raw[u], u * P // HALVES)
-        w1_codes = keep.tile([P, H], U32, name="w1_codes", align_bytes=64)
+        w1_grouped = keep.tile([P, PACK, P, PACK], BF16, name="w1_grouped", tag="page0", align_bytes=64)
+        nc.vector.tensor_copy(
+            w1_grouped[:].rearrange("p t m j -> p m j t"), w1_raw[:].rearrange("p j (m t) -> p m j t", t=PACK)
+        )
+        w1_codes = keep.tile([P, H], U32, name="w1_codes", tag="page3", align_bytes=64)
         w1_plane = keep.tile([P, H], U8, name="w1_plane", align_bytes=64)
+        nc.vector.quantize_mx(
+            out=w1_codes[:].bitcast(FP8X4), scales=w1_plane[:], in_=w1_grouped[:].rearrange("p t m j -> p (t m j)")
+        )
+
+        y_banks = [psum.tile([P, S], F32, name=f"y_bank{t}", tag=f"bank{t}") for t in range(PACK)]
+        x_codes = []
+        for c in range(2):
+            codes = keep.tile([P, CHUNK], U32, name=f"x_codes{c}", align_bytes=64)
+            nc.vector.tensor_copy(codes[:], word_table[:].indirect(entries(offs_sb, c)))
+            x_codes.append(codes)
+        for t0 in range(0, PACK, 2):
+            for c in range(2):
+                for t in (t0, t0 + 1):
+                    nc.tensor.matmul_mx(
+                        out=y_banks[t][:, c * CHUNK : (c + 1) * CHUNK],
+                        lhsT=w1_codes[:, t * P : (t + 1) * P].bitcast(FP8X4),
+                        lhsT_scale=w1_plane[:, t * P : (t + 1) * P],
+                        rhs=x_codes[c][:].bitcast(FP8X4),
+                        rhs_scale=x_plane[:, c * CHUNK : (c + 1) * CHUNK],
+                        start=True,
+                        stop=True,
+                    )
         y = []
         for t in range(PACK):
-            cols = slice(t * P, (t + 1) * P)
-            nc.vector.quantize_mx(
-                out=w1_codes[:, cols].bitcast(FP8X4),
-                scales=w1_plane[:, cols],
-                in_=w1_grouped[:, t].rearrange("p m j -> p (m j)"),
-            )
-        for t in range(PACK):
-            cols = slice(t * P, (t + 1) * P)
-            bank = psum.tile([P, S], F32, name=f"y_bank{t}", tag=f"bank{t}")
-            nc.tensor.matmul_mx(
-                out=bank[:],
-                lhsT=w1_codes[:, cols].bitcast(FP8X4),
-                lhsT_scale=w1_plane[:, cols],
-                rhs=x_codes[:].bitcast(FP8X4),
-                rhs_scale=x_plane[:],
-                start=True,
-                stop=True,
-            )
             y_t = keep.tile([P, S], F32, name=f"y{t}")
             if t == 0:
-                nc.scalar.copy(y_t[:], bank[:])
+                nc.scalar.copy(y_t[:], y_banks[t][:])
             else:
-                nc.vector.tensor_copy(y_t[:], bank[:])
+                nc.vector.tensor_copy(y_t[:], y_banks[t][:])
             y.append(y_t)
 
-        w2_raw = keep.tile([P, PACK, N], F32, name="w2_raw", tag="words_w2")
+        w2_raw = keep.tile([P, PACK, N], F32, name="w2_raw", tag="weights")
         nc.sync.dma_start(w2_raw[:], w2.rearrange("(p j) c -> p j c", j=PACK))
         mem_rows = mem.rearrange("(b t r) u -> t b r u", t=PACK, r=8)
         out_rows = out.rearrange("(b t r) u -> t b r u", t=PACK, r=8)
         page = []
         for t in range(PACK):
-            tile = keep.tile([P, U], F32, name=f"page{t}", tag=f"stage{t}", align_bytes=64)
+            tile = keep.tile([P, U], F32, name=f"page{t}", tag=f"page{t}", align_bytes=64)
             nc.sync.dma_start(tile[:], mem_rows[t])
             page.append(tile)
 
-        diff = [keep.tile([P, PACK, CHUNK], F32, name=f"diff{c}") for c in range(2)]
+        def slot(name, tag):
+            return keep.tile([P, CHUNK], F32, name=name, tag=tag, align_bytes=64)
 
-        def fetch_pair(c, t):
-            if c == 1 and t == 0:
-                both = keep.tile([P, 2, CHUNK], F32, name="pair1_0", tag="z0", align_bytes=64)
-                a, b = both[:, 0, :], both[:, 1, :]
-            elif c == 1:
-                a = keep.tile([P, CHUNK], F32, name=f"a{c}_{t}", tag=f"th0_{t - 1}")[:]
-                b = keep.tile([P, CHUNK], F32, name=f"b{c}_{t}", tag=f"old_half0_{t - 1}")[:]
-            else:
-                a = keep.tile([P, CHUNK], F32, name=f"a{c}_{t}", tag=f"a0_{t}", align_bytes=64)[:]
-                b = keep.tile([P, CHUNK], F32, name=f"b{c}_{t}")[:]
-            nc.scalar.activation(a, y[t][:].indirect(entries(n1_sb, c)), ACT.Copy)
-            nc.scalar.activation(b, y[t][:].indirect(entries(n2_sb, c)), ACT.Copy)
+        diff = [keep.tile([P, PACK, CHUNK], F32, name=f"diff{c}", tag=f"diff{c}", align_bytes=64) for c in range(2)]
+
+        def fetch_pair(c, t, a, b, on_vector):
+            for dst, offsets in ((a, n1_sb), (b, n2_sb)):
+                looked_up = y[t][:].indirect(entries(offsets, c))
+                if on_vector:
+                    nc.vector.tensor_copy(dst, looked_up)
+                else:
+                    nc.scalar.activation(dst, looked_up, ACT.Copy)
             return a, b
 
         def less_smaller(c, t, a, b):
-            low = keep.tile([P, CHUNK], F32, name=f"low{c}_{t}", tag=f"low{c}_{t}")
+            low = keep.tile([P, CHUNK], F32, name=f"low{c}_{t}")
             nc.vector.tensor_tensor(low[:], a, b, ALU.min)
             nc.vector.tensor_tensor(diff[c][:, t, :], y[t][:, c * CHUNK : (c + 1) * CHUNK], low[:], ALU.subtract)
 
-        def quantise_z(c):
-            z = keep.tile([P, CHUNK, PACK], BF16, name=f"z{c}", tag=f"z{c}", align_bytes=64)
+        def quantise_z(c, tag):
+            z = keep.tile([P, CHUNK, PACK], BF16, name=f"z{c}", tag=tag, align_bytes=64)
             nc.vector.tensor_tensor(
                 z[:].rearrange("p (c i) t -> p c t i", i=4),
                 diff[c][:].rearrange("p t (c i) -> p c t i", i=4),
@@ -158,11 +150,10 @@ def tile_picked_hashunderpaget_none_p_kernel(
             return z_codes, z_plane
 
         def quantise_w2(t):
-            grouped = keep.tile([P, P, PACK], BF16, name=f"w2_grouped{t}", tag=f"a0_{t}" if t else "w2_first", align_bytes=64)
+            grouped = keep.tile([P, P, PACK], BF16, name=f"w2_grouped{t}", tag=f"first{t}", align_bytes=64)
             codes = keep.tile([P, P], U32, name=f"w2_codes{t}", align_bytes=64)
             plane = keep.tile([P, P], U8, name=f"w2_plane{t}", align_bytes=64)
-            copy = nc.vector.tensor_copy if t == 0 else nc.scalar.copy
-            copy(
+            nc.scalar.copy(
                 grouped[:].rearrange("p (b s i) j -> p b s j i", s=2, i=4),
                 w2_raw[:].rearrange("p j (b t s i) -> p t b s j i", t=PACK, s=2, i=4)[:, t],
             )
@@ -171,53 +162,76 @@ def tile_picked_hashunderpaget_none_p_kernel(
             )
             return codes, plane
 
-        def fetch_old(c, t):
-            old_half = keep.tile([P, CHUNK], F32, name=f"old_half{c}_{t}", tag=f"old_half0_{t}" if c == 0 else ["th0_2", "old_half0_2", "low1_3", "th0_3"][t])
+        def fetch_old(c, t, tag):
+            old_half = slot(f"old_half{c}_{t}", tag)
             nc.scalar.activation(old_half[:], page[t][:].indirect(entries(n3_sb, c)), ACT.Copy, scale=0.5)
             return old_half
 
-        def gate(c, t, w2_q, z_q):
+        def gate(c, t, z_q, tag_th, tag_gated):
             bank = psum.tile([P, CHUNK], F32, name=f"h_bank{c}_{t}", tag=f"bank{(PACK * (c + 1) + t) % 8}")
             nc.tensor.matmul_mx(
                 out=bank[:],
-                lhsT=w2_q[0][:].bitcast(FP8X4),
-                lhsT_scale=w2_q[1][:],
+                lhsT=w2_q[t][0][:].bitcast(FP8X4),
+                lhsT_scale=w2_q[t][1][:],
                 rhs=z_q[0][:].bitcast(FP8X4),
                 rhs_scale=z_q[1][:],
                 start=True,
                 stop=True,
             )
-            th = keep.tile([P, CHUNK], F32, name=f"th{c}_{t}", tag=f"th{c}_{t}")
-            gated = keep.tile([P, CHUNK], F32, name=f"gated{c}_{t}")
+            th = slot(f"th{c}_{t}", tag_th)
+            gated = slot(f"gated{c}_{t}", tag_gated)
             nc.scalar.activation(gated[:], bank[:], ACT.Silu)
             nc.scalar.activation(th[:], bank[:], ACT.Tanh, scale=-0.5)
             return th, gated
 
-        def write_page(c, t, old_half, th, gated):
-            kept = keep.tile([P, CHUNK], F32, name=f"kept{c}_{t}")
+        def keep_old(c, t, old_half, th, tag):
+            kept = slot(f"kept{c}_{t}", tag)
             nc.vector.scalar_tensor_tensor(kept[:], th[:], 1.0, old_half[:], ALU.add, ALU.mult)
+            return kept
+
+        def write_page(c, t, kept, gated):
             nc.vector.tensor_tensor(page[t][:].indirect(entries(n3_sb, c)), kept[:], gated[:], ALU.add)
 
-        w2_q = []
         for t in range(PACK):
-            less_smaller(0, t, *fetch_pair(0, t))
-            if t == 1:
-                w2_q.append(quantise_w2(0))
-        z_first = quantise_z(0)
+            a = slot(f"a0_{t}", f"first{t}")
+            b = slot(f"b0_{t}", f"second{t}")
+            less_smaller(0, t, *fetch_pair(0, t, a[:], b[:], t == PACK - 1))
+        w2_q = [quantise_w2(0)]
+        z_first = quantise_z(0, "z0")
+        both = keep.tile([P, 2, CHUNK], F32, name="pair1_0", tag="z0", align_bytes=64)
+        less_smaller(1, 0, *fetch_pair(1, 0, both[:, 0, :], both[:, 1, :], True))
         for t in range(1, PACK):
             w2_q.append(quantise_w2(t))
 
-        olds = {}
-        gates = {}
+        def tags(t):
+            ring = [f"y{t % 2}", f"z{t % 2}"]
+            return f"ring_x{t % 2}", "ring_" + ring[t // 2], "ring_" + ring[1 - t // 2]
+
+        def prepare(t):
+            tag_th, tag_old, tag_gated = tags(t)
+            old_half = fetch_old(0, t, tag_old)
+            th, gated = gate(0, t, z_first, tag_th, tag_gated)
+            return old_half, th, gated
+
+        ready = [prepare(0), prepare(1)]
+        for t in range(PACK - 1):
+            old_half, th, gated = ready[t]
+            tag_th, tag_old, tag_gated = tags(t)
+            kept = keep_old(0, t, old_half, th, f"kept0_{t}")
+            a = slot(f"a1_{t + 1}", tag_th)
+            b = slot(f"b1_{t + 1}", tag_old)
+            pair = fetch_pair(1, t + 1, a[:], b[:], False)
+            write_page(0, t, kept, gated)
+            less_smaller(1, t + 1, *pair)
+            if t + 2 < PACK:
+                ready.append(prepare(t + 2))
+        olds = [fetch_old(1, t, tag) for t, tag in enumerate(tags(2))]
+
+        z_second = quantise_z(1, "z1")
+        old_half, th, gated = ready[PACK - 1]
+        write_page(0, PACK - 1, keep_old(0, PACK - 1, old_half, th, "diff1"), gated)
+        olds.append(fetch_old(1, PACK - 1, "last_old"))
         for t in range(PACK):
-            olds[t] = fetch_old(0, t)
-            gates[t] = gate(0, t, w2_q[t], z_first)
-            pair = fetch_pair(1, t)
-            if t < PACK - 1:
-                write_page(0, t, olds[t], *gates[t])
-            less_smaller(1, t, *pair)
-        z_second = quantise_z(1)
-        write_page(0, PACK - 1, olds[PACK - 1], *gates[PACK - 1])
-        for t in range(PACK):
-            write_page(1, t, fetch_old(1, t), *gate(1, t, w2_q[t], z_second))
+            th, gated = gate(1, t, z_second, f"th1_{t}", f"gated1_{t}")
+            write_page(1, t, keep_old(1, t, olds[t], th, f"kept1_{t}"), gated)
             nc.sync.dma_start(out_rows[t], page[t][:])

@@ -78,32 +78,28 @@ def tile_picked_hashunderpaget_none_p_kernel(
             out=w1_codes[:].bitcast(FP8X4), scales=w1_plane[:], in_=w1_grouped[:].rearrange("p t m j -> p (t m j)")
         )
 
-        y_banks = [psum.tile([P, S], F32, name=f"y_bank{t}", tag=f"bank{t}") for t in range(PACK)]
         x_codes = []
         for c in range(2):
             codes = keep.tile([P, CHUNK], U32, name=f"x_codes{c}", align_bytes=64)
             nc.vector.tensor_copy(codes[:], word_table[:].indirect(entries(offs_sb, c)))
             x_codes.append(codes)
+        y = [keep.tile([P, S], F32, name=f"y{t}") for t in range(PACK)]
         for t0 in range(0, PACK, 2):
-            for c in range(2):
-                for t in (t0, t0 + 1):
-                    nc.tensor.matmul_mx(
-                        out=y_banks[t][:, c * CHUNK : (c + 1) * CHUNK],
-                        lhsT=w1_codes[:, t * P : (t + 1) * P].bitcast(FP8X4),
-                        lhsT_scale=w1_plane[:, t * P : (t + 1) * P],
-                        rhs=x_codes[c][:].bitcast(FP8X4),
-                        rhs_scale=x_plane[:, c * CHUNK : (c + 1) * CHUNK],
-                        start=True,
-                        stop=True,
-                    )
-        y = []
-        for t in range(PACK):
-            y_t = keep.tile([P, S], F32, name=f"y{t}")
-            if t == 0:
-                nc.scalar.copy(y_t[:], y_banks[t][:])
-            else:
-                nc.vector.tensor_copy(y_t[:], y_banks[t][:])
-            y.append(y_t)
+            order = [(t, c) for c in range(2) for t in (t0, t0 + 1)]
+            for t, c in order if t0 == 0 else sorted(order):
+                cols = slice(c * CHUNK, (c + 1) * CHUNK)
+                bank = psum.tile([P, CHUNK], F32, name=f"y_bank{t}_{c}", tag=f"bank{2 * t + c}")
+                nc.tensor.matmul_mx(
+                    out=bank[:],
+                    lhsT=w1_codes[:, t * P : (t + 1) * P].bitcast(FP8X4),
+                    lhsT_scale=w1_plane[:, t * P : (t + 1) * P],
+                    rhs=x_codes[c][:].bitcast(FP8X4),
+                    rhs_scale=x_plane[:, cols],
+                    start=True,
+                    stop=True,
+                )
+                copy = nc.scalar.copy if t == 0 else nc.vector.tensor_copy
+                copy(y[t][:, cols], bank[:])
 
         w2_raw = keep.tile([P, PACK, N], F32, name="w2_raw", tag="weights")
         nc.sync.dma_start(w2_raw[:], w2.rearrange("(p j) c -> p j c", j=PACK))
@@ -130,7 +126,7 @@ def tile_picked_hashunderpaget_none_p_kernel(
             return a, b
 
         def less_smaller(c, t, a, b):
-            low = keep.tile([P, CHUNK], F32, name=f"low{c}_{t}")
+            low = slot(f"low{c}_{t}", "z0" if (c, t) == (1, 0) else f"low{c}_{t}")
             nc.vector.tensor_tensor(low[:], a, b, ALU.min)
             nc.vector.tensor_tensor(diff[c][:, t, :], y[t][:, c * CHUNK : (c + 1) * CHUNK], low[:], ALU.subtract)
 
@@ -149,89 +145,124 @@ def tile_picked_hashunderpaget_none_p_kernel(
             )
             return z_codes, z_plane
 
-        def quantise_w2(t):
-            grouped = keep.tile([P, P, PACK], BF16, name=f"w2_grouped{t}", tag=f"first{t}", align_bytes=64)
-            codes = keep.tile([P, P], U32, name=f"w2_codes{t}", align_bytes=64)
-            plane = keep.tile([P, P], U8, name=f"w2_plane{t}", align_bytes=64)
-            nc.scalar.copy(
-                grouped[:].rearrange("p (b s i) j -> p b s j i", s=2, i=4),
-                w2_raw[:].rearrange("p j (b t s i) -> p t b s j i", t=PACK, s=2, i=4)[:, t],
-            )
+        def quantise_w2(ts, tag):
+            grouped = keep.tile([P, len(ts), P, PACK], BF16, name=f"w2_grouped{ts[0]}", tag=tag, align_bytes=64)
+            codes = keep.tile([P, len(ts), P], U32, name=f"w2_codes{ts[0]}", align_bytes=64)
+            plane = keep.tile([P, len(ts), P], U8, name=f"w2_plane{ts[0]}", align_bytes=64)
+            for a, t in enumerate(ts):
+                copy = nc.vector.tensor_copy if t == PACK - 1 else nc.scalar.copy
+                copy(
+                    grouped[:, a].rearrange("p (b s i) j -> p b s j i", s=2, i=4),
+                    w2_raw[:].rearrange("p j (b t s i) -> p t b s j i", t=PACK, s=2, i=4)[:, t],
+                )
             nc.vector.quantize_mx(
-                out=codes[:].bitcast(FP8X4), scales=plane[:], in_=grouped[:].rearrange("p m j -> p (m j)")
+                out=codes[:].rearrange("p a m -> p (a m)").bitcast(FP8X4),
+                scales=plane[:].rearrange("p a m -> p (a m)"),
+                in_=grouped[:].rearrange("p a m j -> p (a m j)"),
             )
-            return codes, plane
+            return [(codes[:, a], plane[:, a]) for a in range(len(ts))]
 
-        def fetch_old(c, t, tag):
-            old_half = slot(f"old_half{c}_{t}", tag)
-            nc.scalar.activation(old_half[:], page[t][:].indirect(entries(n3_sb, c)), ACT.Copy, scale=0.5)
-            return old_half
+        def fetch_old(c, t, old_half):
+            nc.scalar.activation(old_half, page[t][:].indirect(entries(n3_sb, c)), ACT.Copy, scale=0.5)
 
-        def gate(c, t, z_q, tag_th, tag_gated):
-            bank = psum.tile([P, CHUNK], F32, name=f"h_bank{c}_{t}", tag=f"bank{(PACK * (c + 1) + t) % 8}")
+        def product(t, z_q, h):
             nc.tensor.matmul_mx(
-                out=bank[:],
-                lhsT=w2_q[t][0][:].bitcast(FP8X4),
-                lhsT_scale=w2_q[t][1][:],
+                out=h,
+                lhsT=w2_q[t][0].bitcast(FP8X4),
+                lhsT_scale=w2_q[t][1],
                 rhs=z_q[0][:].bitcast(FP8X4),
                 rhs_scale=z_q[1][:],
                 start=True,
                 stop=True,
             )
-            th = slot(f"th{c}_{t}", tag_th)
-            gated = slot(f"gated{c}_{t}", tag_gated)
-            nc.scalar.activation(gated[:], bank[:], ACT.Silu)
-            nc.scalar.activation(th[:], bank[:], ACT.Tanh, scale=-0.5)
-            return th, gated
 
-        def keep_old(c, t, old_half, th, tag):
-            kept = slot(f"kept{c}_{t}", tag)
-            nc.vector.scalar_tensor_tensor(kept[:], th[:], 1.0, old_half[:], ALU.add, ALU.mult)
-            return kept
+        def tanh_half(th, h):
+            nc.scalar.activation(th, h, ACT.Tanh, scale=-0.5)
+
+        def silu(gated, h):
+            nc.scalar.activation(gated, h, ACT.Silu)
+
+        def keep_old(kept, old_half, th):
+            nc.vector.scalar_tensor_tensor(kept, th, 1.0, old_half, ALU.add, ALU.mult)
 
         def write_page(c, t, kept, gated):
-            nc.vector.tensor_tensor(page[t][:].indirect(entries(n3_sb, c)), kept[:], gated[:], ALU.add)
+            nc.vector.tensor_tensor(page[t][:].indirect(entries(n3_sb, c)), kept, gated, ALU.add)
 
         for t in range(PACK):
             a = slot(f"a0_{t}", f"first{t}")
             b = slot(f"b0_{t}", f"second{t}")
-            less_smaller(0, t, *fetch_pair(0, t, a[:], b[:], t == PACK - 1))
-        w2_q = [quantise_w2(0)]
+            less_smaller(0, t, *fetch_pair(0, t, a[:], b[:], t == 1))
+        w2_q = quantise_w2([0], "first2")
+        a = slot("a1_0", "first0")
+        b = slot("b1_0", "second0")
+        pair = fetch_pair(1, 0, a[:], b[:], False)
         z_first = quantise_z(0, "z0")
-        both = keep.tile([P, 2, CHUNK], F32, name="pair1_0", tag="z0", align_bytes=64)
-        less_smaller(1, 0, *fetch_pair(1, 0, both[:, 0, :], both[:, 1, :], True))
-        for t in range(1, PACK):
-            w2_q.append(quantise_w2(t))
+        less_smaller(1, 0, *pair)
+        w2_q.extend(quantise_w2([1, 2, 3], "low0_3"))
 
         def tags(t):
             ring = [f"y{t % 2}", f"z{t % 2}"]
             return f"ring_x{t % 2}", "ring_" + ring[t // 2], "ring_" + ring[1 - t // 2]
 
+        banks, olds, ths, gateds = {}, {}, {}, {}
+        last = PACK - 1
+
         def prepare(t):
             tag_th, tag_old, tag_gated = tags(t)
-            old_half = fetch_old(0, t, tag_old)
-            th, gated = gate(0, t, z_first, tag_th, tag_gated)
-            return old_half, th, gated
+            olds[t] = slot(f"old0_{t}", tag_old)
+            fetch_old(0, t, olds[t][:])
+            banks[t] = psum.tile([P, CHUNK], F32, name=f"h_bank0_{t}", tag=f"bank{PACK + t}")
+            product(t, z_first, banks[t][:])
+            ths[t] = slot(f"th0_{t}", tag_th)
+            tanh_half(ths[t][:], banks[t][:])
 
-        ready = [prepare(0), prepare(1)]
-        for t in range(PACK - 1):
-            old_half, th, gated = ready[t]
+        def first_silu(t, tag):
+            gateds[t] = slot(f"gated0_{t}", tag)
+            silu(gateds[t][:], banks[t][:])
+
+        def first_kept(t):
+            kept = slot(f"kept0_{t}", f"kept0_{t}")
+            keep_old(kept[:], olds[t][:], ths[t][:])
+            return kept
+
+        prepare(0)
+        first_silu(0, tags(0)[2])
+        prepare(1)
+        for t in range(last):
             tag_th, tag_old, tag_gated = tags(t)
-            kept = keep_old(0, t, old_half, th, f"kept0_{t}")
+            kept = first_kept(t)
             a = slot(f"a1_{t + 1}", tag_th)
             b = slot(f"b1_{t + 1}", tag_old)
             pair = fetch_pair(1, t + 1, a[:], b[:], False)
-            write_page(0, t, kept, gated)
+            if t + 1 < last:
+                first_silu(t + 1, tags(t + 1)[2])
+            write_page(0, t, kept[:], gateds[t][:])
             less_smaller(1, t + 1, *pair)
             if t + 2 < PACK:
-                ready.append(prepare(t + 2))
-        olds = [fetch_old(1, t, tag) for t, tag in enumerate(tags(2))]
+                prepare(t + 2)
+        kept = first_kept(last)
+        late_olds = [
+            keep.tile([P, 2, CHUNK], F32, name=f"old1_{g}", tag=tags(2)[g], align_bytes=64) for g in range(2)
+        ]
+        for t in range(last):
+            fetch_old(1, t, late_olds[t // 2][:, t % 2, :])
 
         z_second = quantise_z(1, "z1")
-        old_half, th, gated = ready[PACK - 1]
-        write_page(0, PACK - 1, keep_old(0, PACK - 1, old_half, th, "diff1"), gated)
-        olds.append(fetch_old(1, PACK - 1, "last_old"))
-        for t in range(PACK):
-            th, gated = gate(1, t, z_second, f"th1_{t}", f"gated1_{t}")
-            write_page(1, t, keep_old(1, t, olds[t], th, f"kept1_{t}"), gated)
-            nc.sync.dma_start(out_rows[t], page[t][:])
+        first_silu(last, "diff1")
+        write_page(0, last, kept[:], gateds[last][:])
+        for g in range(2):
+            bank = psum.tile([P, 2, CHUNK], F32, name=f"h_bank1_{g}", tag=f"bank{g}")
+            th = keep.tile([P, 2, CHUNK], F32, name=f"th1_{g}")
+            gated = keep.tile([P, 2, CHUNK], F32, name=f"gated1_{g}")
+            kept = keep.tile([P, 2, CHUNK], F32, name=f"kept1_{g}")
+            for a in range(2):
+                product(2 * g + a, z_second, bank[:, a, :])
+            tanh_half(th[:], bank[:])
+            silu(gated[:], bank[:])
+            if g == 0:
+                fetch_old(1, last, late_olds[1][:, 1, :])
+            keep_old(kept[:], late_olds[g][:], th[:])
+            for a in range(2):
+                t = 2 * g + a
+                write_page(1, t, kept[:, a, :], gated[:, a, :])
+                nc.sync.dma_start(out_rows[t], page[t][:])

@@ -18,8 +18,12 @@ ACT = mybir.ActivationFunctionType
 P = 128
 PACK = 4
 GROUP = 16
-CHUNK = 256
-HALVES = 2
+BLOCK_ROWS = 8
+BLOCKS = P // BLOCK_ROWS
+QUADRANT = 32
+CHUNK = S // 2
+RUN = 4
+LAST = PACK - 1
 
 
 def tile_picked_hashunderpaget_none_p_kernel(
@@ -36,8 +40,14 @@ def tile_picked_hashunderpaget_none_p_kernel(
             nc.sync.dma_start(tile[:], src)
             return tile
 
-        def entries(tile, c):
-            return tile[:, c * CHUNK // GROUP : (c + 1) * CHUNK // GROUP]
+        def entries(list_tile, c):
+            return list_tile[:, c * CHUNK // GROUP : (c + 1) * CHUNK // GROUP]
+
+        def places(c):
+            return slice(c * CHUNK, (c + 1) * CHUNK)
+
+        def chunk_tile(name, tag):
+            return keep.tile([P, CHUNK], F32, name=name, tag=tag, align_bytes=64)
 
         warm_in = keep.tile([P, 1], F32, name="warm_in")
         warm_out = keep.tile([P, 1], F32, name="warm_out")
@@ -45,9 +55,10 @@ def tile_picked_hashunderpaget_none_p_kernel(
         nc.scalar.activation(warm_out[:], warm_in[:], ACT.Silu)
 
         offs_sb = load_list(offs, "offs_sb")
-        scale_table = keep.tile([P, T], U8, name="scale_table", tag="scales_gain")
+        scale_table = keep.tile([P, T], U8, name="scale_table", tag="scales_then_gain")
         nc.sync.dma_start(
-            scale_table[:].bitcast(I32), x_scales[0].bitcast(I32).unsqueeze(1).to_broadcast([16, 8, T // 4])
+            scale_table[:].bitcast(I32),
+            x_scales[0].bitcast(I32).unsqueeze(1).to_broadcast([BLOCKS, BLOCK_ROWS, T // 4]),
         )
         n1_sb = load_list(n1, "n1_sb")
         w1_raw = keep.tile([P, PACK, H], F32, name="w1_raw", tag="weights")
@@ -61,12 +72,20 @@ def tile_picked_hashunderpaget_none_p_kernel(
         nc.vector.tensor_copy(picked_bytes[:], scale_table[:].indirect(offs_sb[:]))
         x_plane = keep.tile([P, S], U8, name="x_plane", align_bytes=64)
         nc.vector.memset(x_plane[:].bitcast(I32), 0)
-        for i in range(4):
+        for i in range(QUADRANT // BLOCK_ROWS):
             nc.scalar.dma_start(
-                x_plane[:].bitcast(I32)[i:P:32, :], picked_bytes[:].bitcast(I32)[8 * i : P : 32, :]
+                x_plane[:].bitcast(I32)[i:P:QUADRANT, :],
+                picked_bytes[:].bitcast(I32)[BLOCK_ROWS * i : P : QUADRANT, :],
             )
-        gain = keep.tile([P, PACK], F32, name="gain", tag="scales_gain")
+
+        gain = keep.tile([P, PACK], F32, name="gain", tag="scales_then_gain")
         nc.sync.dma_start(gain[:], gn.rearrange("(p t) o -> p (t o)", t=PACK))
+        gain_size = keep.tile([P, PACK], F32, name="gain_size")
+        gain_sign = keep.tile([P, PACK], F32, name="gain_sign")
+        minus_sign = keep.tile([P, PACK], F32, name="minus_sign")
+        nc.scalar.activation(gain_size[:], gain[:], ACT.Abs)
+        nc.scalar.activation(gain_sign[:], gain[:], ACT.Sign)
+        nc.scalar.activation(minus_sign[:], gain[:], ACT.Sign, scale=-1.0)
 
         w1_grouped = keep.tile([P, PACK, P, PACK], BF16, name="w1_grouped", tag="page0", align_bytes=64)
         nc.vector.tensor_copy(
@@ -83,61 +102,80 @@ def tile_picked_hashunderpaget_none_p_kernel(
             codes = keep.tile([P, CHUNK], U32, name=f"x_codes{c}", align_bytes=64)
             nc.vector.tensor_copy(codes[:], word_table[:].indirect(entries(offs_sb, c)))
             x_codes.append(codes)
-        y = [keep.tile([P, S], F32, name=f"y{t}") for t in range(PACK)]
-        for t0 in range(0, PACK, 2):
-            order = [(t, c) for c in range(2) for t in (t0, t0 + 1)]
-            for t, c in order if t0 == 0 else sorted(order):
-                cols = slice(c * CHUNK, (c + 1) * CHUNK)
-                bank = psum.tile([P, CHUNK], F32, name=f"y_bank{t}_{c}", tag=f"bank{2 * t + c}")
-                nc.tensor.matmul_mx(
-                    out=bank[:],
-                    lhsT=w1_codes[:, t * P : (t + 1) * P].bitcast(FP8X4),
-                    lhsT_scale=w1_plane[:, t * P : (t + 1) * P],
-                    rhs=x_codes[c][:].bitcast(FP8X4),
-                    rhs_scale=x_plane[:, cols],
-                    start=True,
-                    stop=True,
-                )
-                copy = nc.scalar.copy if t == 0 else nc.vector.tensor_copy
-                copy(y[t][:, cols], bank[:])
+        sized = [keep.tile([P, S], F32, name=f"sized{t}") for t in range(PACK)]
+
+        def first_product(t, c):
+            bank = psum.tile([P, CHUNK], F32, name=f"y_bank{t}_{c}", tag=f"bank{2 * t + c}")
+            nc.tensor.matmul_mx(
+                out=bank[:],
+                lhsT=w1_codes[:, t * P : (t + 1) * P].bitcast(FP8X4),
+                lhsT_scale=w1_plane[:, t * P : (t + 1) * P],
+                rhs=x_codes[c][:].bitcast(FP8X4),
+                rhs_scale=x_plane[:, places(c)],
+                start=True,
+                stop=True,
+            )
+            if t == 0:
+                nc.scalar.activation(sized[t][:, places(c)], bank[:], ACT.Copy, scale=gain_size[:, t : t + 1])
+            else:
+                nc.vector.tensor_scalar(sized[t][:, places(c)], bank[:], gain_size[:, t : t + 1], None, ALU.mult)
+
+        for c in range(2):
+            for t in range(2):
+                first_product(t, c)
+        for t in range(2, PACK):
+            for c in range(2):
+                first_product(t, c)
 
         w2_raw = keep.tile([P, PACK, N], F32, name="w2_raw", tag="weights")
         nc.sync.dma_start(w2_raw[:], w2.rearrange("(p j) c -> p j c", j=PACK))
-        mem_rows = mem.rearrange("(b t r) u -> t b r u", t=PACK, r=8)
-        out_rows = out.rearrange("(b t r) u -> t b r u", t=PACK, r=8)
+        mem_rows = mem.rearrange("(b t r) u -> t b r u", t=PACK, r=BLOCK_ROWS)
+        out_rows = out.rearrange("(b t r) u -> t b r u", t=PACK, r=BLOCK_ROWS)
         page = []
         for t in range(PACK):
             tile = keep.tile([P, U], F32, name=f"page{t}", tag=f"page{t}", align_bytes=64)
             nc.sync.dma_start(tile[:], mem_rows[t])
             page.append(tile)
 
-        def slot(name, tag):
-            return keep.tile([P, CHUNK], F32, name=name, tag=tag, align_bytes=64)
+        diff = keep.tile([P, PACK, CHUNK], F32, name="diff", tag="diff", align_bytes=64)
+        z_rows = keep.tile([P, PACK, CHUNK], BF16, name="z_rows", tag="z_rows", align_bytes=64)
 
-        diff = [keep.tile([P, PACK, CHUNK], F32, name=f"diff{c}", tag=f"diff{c}", align_bytes=64) for c in range(2)]
-
-        def fetch_pair(c, t, a, b, on_vector):
-            for dst, offsets in ((a, n1_sb), (b, n2_sb)):
-                looked_up = y[t][:].indirect(entries(offsets, c))
+        def fetch_pair(c, t, tag_1, tag_2, on_vector=False):
+            at_1 = chunk_tile(f"at_n1_{c}_{t}", tag_1)
+            at_2 = chunk_tile(f"at_n2_{c}_{t}", tag_2)
+            for dst, list_tile in ((at_1, n1_sb), (at_2, n2_sb)):
+                looked_up = sized[t][:].indirect(entries(list_tile, c))
                 if on_vector:
-                    nc.vector.tensor_copy(dst, looked_up)
+                    nc.vector.tensor_copy(dst[:], looked_up)
                 else:
-                    nc.scalar.activation(dst, looked_up, ACT.Copy)
-            return a, b
+                    nc.scalar.activation(dst[:], looked_up, ACT.Copy)
+            return at_1, at_2
 
-        def less_smaller(c, t, a, b):
-            low = slot(f"low{c}_{t}", "z0" if (c, t) == (1, 0) else f"low{c}_{t}")
-            nc.vector.tensor_tensor(low[:], a, b, ALU.min)
-            nc.vector.tensor_tensor(diff[c][:, t, :], y[t][:, c * CHUNK : (c + 1) * CHUNK], low[:], ALU.subtract)
+        def smaller(c, t, pair, tag):
+            low = chunk_tile(f"low{c}_{t}", tag)
+            nc.vector.tensor_tensor(low[:], pair[0][:], pair[1][:], ALU.min)
+            return low
 
-        def quantise_z(c, tag):
-            z = keep.tile([P, CHUNK, PACK], BF16, name=f"z{c}", tag=tag, align_bytes=64)
-            nc.vector.tensor_tensor(
-                z[:].rearrange("p (c i) t -> p c t i", i=4),
-                diff[c][:].rearrange("p t (c i) -> p c t i", i=4),
-                gain[:].unsqueeze(1).unsqueeze(3).to_broadcast([P, CHUNK // 4, PACK, 4]),
-                ALU.mult,
+        def subtract_first(t, low):
+            nc.vector.tensor_tensor(diff[:, t, :], sized[t][:, places(0)], low[:], ALU.subtract)
+
+        def subtract_second(t, low):
+            nc.vector.scalar_tensor_tensor(
+                z_rows[:, t, :], low[:], minus_sign[:, t : t + 1], signed[:, t, :], ALU.mult, ALU.add
             )
+
+        def quantise_z(c):
+            z = keep.tile([P, CHUNK, PACK], BF16, name=f"z{c}", tag=f"z{c}", align_bytes=64)
+            woven = z[:].rearrange("p (n i) t -> p n t i", i=RUN)
+            if c == 0:
+                nc.vector.tensor_tensor(
+                    woven,
+                    diff[:].rearrange("p t (n i) -> p n t i", i=RUN),
+                    gain_sign[:].unsqueeze(1).unsqueeze(3).to_broadcast([P, CHUNK // RUN, PACK, RUN]),
+                    ALU.mult,
+                )
+            else:
+                nc.vector.tensor_copy(woven, z_rows[:].rearrange("p t (n i) -> p n t i", i=RUN))
             z_codes = keep.tile([P, CHUNK], U32, name=f"z_codes{c}", align_bytes=64)
             z_plane = keep.tile([P, CHUNK], U8, name=f"z_plane{c}", align_bytes=64)
             nc.vector.quantize_mx(
@@ -145,33 +183,34 @@ def tile_picked_hashunderpaget_none_p_kernel(
             )
             return z_codes, z_plane
 
-        def quantise_w2(ts, tag):
-            grouped = keep.tile([P, len(ts), P, PACK], BF16, name=f"w2_grouped{ts[0]}", tag=tag, align_bytes=64)
-            codes = keep.tile([P, len(ts), P], U32, name=f"w2_codes{ts[0]}", align_bytes=64)
-            plane = keep.tile([P, len(ts), P], U8, name=f"w2_plane{ts[0]}", align_bytes=64)
-            for a, t in enumerate(ts):
-                copy = nc.vector.tensor_copy if t == PACK - 1 else nc.scalar.copy
+        def quantise_w2(tiles, tag, copy):
+            count = len(tiles)
+            grouped = keep.tile([P, count, P, PACK], BF16, name=f"w2_grouped{tiles[0]}", tag=tag, align_bytes=64)
+            codes = keep.tile([P, count, P], U32, name=f"w2_codes{tiles[0]}", align_bytes=64)
+            plane = keep.tile([P, count, P], U8, name=f"w2_plane{tiles[0]}", align_bytes=64)
+            halves = BLOCK_ROWS // RUN
+            for a, t in enumerate(tiles):
                 copy(
-                    grouped[:, a].rearrange("p (b s i) j -> p b s j i", s=2, i=4),
-                    w2_raw[:].rearrange("p j (b t s i) -> p t b s j i", t=PACK, s=2, i=4)[:, t],
+                    grouped[:, a].rearrange("p (b s i) j -> p b s j i", s=halves, i=RUN),
+                    w2_raw[:].rearrange("p j (b t s i) -> p t b s j i", t=PACK, s=halves, i=RUN)[:, t],
                 )
             nc.vector.quantize_mx(
                 out=codes[:].rearrange("p a m -> p (a m)").bitcast(FP8X4),
                 scales=plane[:].rearrange("p a m -> p (a m)"),
                 in_=grouped[:].rearrange("p a m j -> p (a m j)"),
             )
-            return [(codes[:, a], plane[:, a]) for a in range(len(ts))]
+            return [(codes[:, a], plane[:, a]) for a in range(count)]
 
         def fetch_old(c, t, old_half):
             nc.scalar.activation(old_half, page[t][:].indirect(entries(n3_sb, c)), ACT.Copy, scale=0.5)
 
-        def product(t, z_q, h):
+        def second_product(t, z_quantised, h):
             nc.tensor.matmul_mx(
                 out=h,
-                lhsT=w2_q[t][0].bitcast(FP8X4),
-                lhsT_scale=w2_q[t][1],
-                rhs=z_q[0][:].bitcast(FP8X4),
-                rhs_scale=z_q[1][:],
+                lhsT=w2_quantised[t][0].bitcast(FP8X4),
+                lhsT_scale=w2_quantised[t][1],
+                rhs=z_quantised[0][:].bitcast(FP8X4),
+                rhs_scale=z_quantised[1][:],
                 start=True,
                 stop=True,
             )
@@ -189,80 +228,76 @@ def tile_picked_hashunderpaget_none_p_kernel(
             nc.vector.tensor_tensor(page[t][:].indirect(entries(n3_sb, c)), kept, gated, ALU.add)
 
         for t in range(PACK):
-            a = slot(f"a0_{t}", f"first{t}")
-            b = slot(f"b0_{t}", f"second{t}")
-            less_smaller(0, t, *fetch_pair(0, t, a[:], b[:], t == 1))
-        w2_q = quantise_w2([0], "first2")
-        a = slot("a1_0", "first0")
-        b = slot("b1_0", "second0")
-        pair = fetch_pair(1, 0, a[:], b[:], False)
-        z_first = quantise_z(0, "z0")
-        less_smaller(1, 0, *pair)
-        w2_q.extend(quantise_w2([1, 2, 3], "low0_3"))
+            pair = fetch_pair(0, t, f"at_n1_{t}", f"at_n2_{t}", on_vector=t == 1)
+            subtract_first(t, smaller(0, t, pair, f"low0_{t}"))
+        w2_quantised = quantise_w2([0], "at_n1_2", nc.scalar.copy)
+        pair = fetch_pair(1, 0, "at_n1_0", "at_n2_0")
+        signed = keep.tile([P, PACK, CHUNK], F32, name="signed", tag="at_n2_3", align_bytes=64)
+        for t in range(PACK):
+            nc.scalar.activation(signed[:, t, :], sized[t][:, places(1)], ACT.Copy, scale=gain_sign[:, t : t + 1])
+        z_first = quantise_z(0)
+        subtract_second(0, smaller(1, 0, pair, "z0"))
+        w2_quantised.extend(quantise_w2(list(range(1, PACK)), "diff", nc.vector.tensor_copy))
 
-        def tags(t):
-            ring = [f"y{t % 2}", f"z{t % 2}"]
-            return f"ring_x{t % 2}", "ring_" + ring[t // 2], "ring_" + ring[1 - t // 2]
+        def ring(t):
+            swap = [f"ring_b{t % 2}", f"ring_c{t % 2}"]
+            return f"ring_a{t % 2}", swap[t // 2], swap[1 - t // 2]
 
-        banks, olds, ths, gateds = {}, {}, {}, {}
-        last = PACK - 1
+        h_first, old_first, th_first, gated_first = {}, {}, {}, {}
 
-        def prepare(t):
-            tag_th, tag_old, tag_gated = tags(t)
-            olds[t] = slot(f"old0_{t}", tag_old)
-            fetch_old(0, t, olds[t][:])
-            banks[t] = psum.tile([P, CHUNK], F32, name=f"h_bank0_{t}", tag=f"bank{PACK + t}")
-            product(t, z_first, banks[t][:])
-            ths[t] = slot(f"th0_{t}", tag_th)
-            tanh_half(ths[t][:], banks[t][:])
+        def prepare_first(t):
+            tag_th, tag_old = ring(t)[:2]
+            old_first[t] = chunk_tile(f"old0_{t}", tag_old)
+            fetch_old(0, t, old_first[t][:])
+            h_first[t] = psum.tile([P, CHUNK], F32, name=f"h_bank0_{t}", tag=f"bank{PACK + t}")
+            second_product(t, z_first, h_first[t][:])
+            th_first[t] = chunk_tile(f"th0_{t}", tag_th)
+            tanh_half(th_first[t][:], h_first[t][:])
 
-        def first_silu(t, tag):
-            gateds[t] = slot(f"gated0_{t}", tag)
-            silu(gateds[t][:], banks[t][:])
+        def silu_first(t, tag):
+            gated_first[t] = chunk_tile(f"gated0_{t}", tag)
+            silu(gated_first[t][:], h_first[t][:])
 
-        def first_kept(t):
-            kept = slot(f"kept0_{t}", f"kept0_{t}")
-            keep_old(kept[:], olds[t][:], ths[t][:])
+        def kept_first(t):
+            kept = chunk_tile(f"kept0_{t}", f"kept0_{t}")
+            keep_old(kept[:], old_first[t][:], th_first[t][:])
             return kept
 
-        prepare(0)
-        first_silu(0, tags(0)[2])
-        prepare(1)
-        for t in range(last):
-            tag_th, tag_old, tag_gated = tags(t)
-            kept = first_kept(t)
-            a = slot(f"a1_{t + 1}", tag_th)
-            b = slot(f"b1_{t + 1}", tag_old)
-            pair = fetch_pair(1, t + 1, a[:], b[:], False)
-            if t + 1 < last:
-                first_silu(t + 1, tags(t + 1)[2])
-            write_page(0, t, kept[:], gateds[t][:])
-            less_smaller(1, t + 1, *pair)
+        prepare_first(0)
+        silu_first(0, ring(0)[2])
+        prepare_first(1)
+        for t in range(LAST):
+            kept = kept_first(t)
+            pair = fetch_pair(1, t + 1, *ring(t)[:2])
+            if t + 1 < LAST:
+                silu_first(t + 1, ring(t + 1)[2])
+            write_page(0, t, kept[:], gated_first[t][:])
+            subtract_second(t + 1, smaller(1, t + 1, pair, f"low1_{t + 1}"))
             if t + 2 < PACK:
-                prepare(t + 2)
-        kept = first_kept(last)
-        late_olds = [
-            keep.tile([P, 2, CHUNK], F32, name=f"old1_{g}", tag=tags(2)[g], align_bytes=64) for g in range(2)
-        ]
-        for t in range(last):
-            fetch_old(1, t, late_olds[t // 2][:, t % 2, :])
+                prepare_first(t + 2)
+        kept = kept_first(LAST)
 
-        z_second = quantise_z(1, "z1")
-        first_silu(last, "diff1")
-        write_page(0, last, kept[:], gateds[last][:])
+        old_second = [keep.tile([P, 2, CHUNK], F32, name="old1_0", tag=ring(2)[0], align_bytes=64)]
+        for t in range(2):
+            fetch_old(1, t, old_second[0][:, t, :])
+        z_second = quantise_z(1)
+        silu_first(LAST, "z_rows")
+        old_second.append(keep.tile([P, 2, CHUNK], F32, name="old1_1", tag="z1", align_bytes=64))
+        fetch_old(1, 2, old_second[1][:, 0, :])
+        write_page(0, LAST, kept[:], gated_first[LAST][:])
         for g in range(2):
-            bank = psum.tile([P, 2, CHUNK], F32, name=f"h_bank1_{g}", tag=f"bank{g}")
-            th = keep.tile([P, 2, CHUNK], F32, name=f"th1_{g}")
-            gated = keep.tile([P, 2, CHUNK], F32, name=f"gated1_{g}")
-            kept = keep.tile([P, 2, CHUNK], F32, name=f"kept1_{g}")
+            h_two = psum.tile([P, 2, CHUNK], F32, name=f"h_bank1_{g}", tag=f"bank{g}")
+            th_two = keep.tile([P, 2, CHUNK], F32, name=f"th1_{g}")
+            gated_two = keep.tile([P, 2, CHUNK], F32, name=f"gated1_{g}")
+            kept_two = keep.tile([P, 2, CHUNK], F32, name=f"kept1_{g}")
             for a in range(2):
-                product(2 * g + a, z_second, bank[:, a, :])
-            tanh_half(th[:], bank[:])
-            silu(gated[:], bank[:])
+                second_product(2 * g + a, z_second, h_two[:, a, :])
+            tanh_half(th_two[:], h_two[:])
+            silu(gated_two[:], h_two[:])
             if g == 0:
-                fetch_old(1, last, late_olds[1][:, 1, :])
-            keep_old(kept[:], late_olds[g][:], th[:])
+                fetch_old(1, LAST, old_second[1][:, 1, :])
+            keep_old(kept_two[:], old_second[g][:], th_two[:])
             for a in range(2):
                 t = 2 * g + a
-                write_page(1, t, kept[:, a, :], gated[:, a, :])
+                write_page(1, t, kept_two[:, a, :], gated_two[:, a, :])
                 nc.sync.dma_start(out_rows[t], page[t][:])

from contextlib import ExitStack

import concourse.mybir as mybir

K, T, S, N, H, U = 512, 2048, 512, 512, 512, 1024
FLOPS = 2 * K * H * S + 2 * H * N * S

F32 = mybir.dt.float32
BF16 = mybir.dt.bfloat16
I32 = mybir.dt.int32
U32 = mybir.dt.uint32
U16 = mybir.dt.uint16
U8 = mybir.dt.uint8
FP8X4 = mybir.dt.float8_e4m3fn_x4
ALU = mybir.AluOpType
ACT = mybir.ActivationFunctionType

P = 128
PACK = 4
GROUP = 16
BLOCK_ROWS = 8
BLOCKS = P // BLOCK_ROWS
QUADRANT = 32
CHUNK = S // 2
RUN = 4
LAST = PACK - 1


def tile_picked_hashunderpaget_none_p_kernel(
    tc, x_words, x_scales, w1, gn, w2, mem, offs, n1, n2, n3, out
):
    nc = tc.nc
    with ExitStack() as ctx:
        lists = ctx.enter_context(tc.tile_pool(name="lists", bufs=1))
        keep = ctx.enter_context(tc.tile_pool(name="keep", bufs=1))
        psum = ctx.enter_context(tc.psum_pool(name="psum", bufs=1))

        def load_list(src, name):
            tile = lists.tile([P, S // GROUP], U16, name=name)
            nc.sync.dma_start(tile[:], src)
            return tile

        def entries(list_tile, c):
            return list_tile[:, c * CHUNK // GROUP : (c + 1) * CHUNK // GROUP]

        def places(c):
            return slice(c * CHUNK, (c + 1) * CHUNK)

        def chunk_tile(name, tag):
            return keep.tile([P, CHUNK], F32, name=name, tag=tag, align_bytes=64)

        warm_in = keep.tile([P, 1], F32, name="warm_in")
        warm_out = keep.tile([P, 1], F32, name="warm_out")
        nc.vector.memset(warm_in[:], 0.0)
        nc.scalar.activation(warm_out[:], warm_in[:], ACT.Silu)

        offs_sb = load_list(offs, "offs_sb")
        scale_table = keep.tile([P, T], U8, name="scale_table", tag="scales_then_gain")
        nc.sync.dma_start(
            scale_table[:].bitcast(I32),
            x_scales[0].bitcast(I32).unsqueeze(1).to_broadcast([BLOCKS, BLOCK_ROWS, T // 4]),
        )
        n1_sb = load_list(n1, "n1_sb")
        w1_raw = keep.tile([P, PACK, H], F32, name="w1_raw", tag="weights")
        nc.sync.dma_start(w1_raw[:], w1.rearrange("(p j) c -> p j c", j=PACK))
        word_table = keep.tile([P, T], U32, name="word_table", tag="page2", align_bytes=64)
        nc.sync.dma_start(word_table[:].bitcast(I32), x_words[0].rearrange("p n t -> p (n t)").bitcast(I32))
        n2_sb = load_list(n2, "n2_sb")
        n3_sb = load_list(n3, "n3_sb")

        picked_bytes = keep.tile([P, S], U8, name="picked_bytes", tag="page1", align_bytes=64)
        nc.vector.tensor_copy(picked_bytes[:], scale_table[:].indirect(offs_sb[:]))
        x_plane = keep.tile([P, S], U8, name="x_plane", align_bytes=64)
        nc.vector.memset(x_plane[:].bitcast(I32), 0)
        for i in range(QUADRANT // BLOCK_ROWS):
            nc.scalar.dma_start(
                x_plane[:].bitcast(I32)[i:P:QUADRANT, :],
                picked_bytes[:].bitcast(I32)[BLOCK_ROWS * i : P : QUADRANT, :],
            )

        gain = keep.tile([P, PACK], F32, name="gain", tag="scales_then_gain")
        nc.sync.dma_start(gain[:], gn.rearrange("(p t) o -> p (t o)", t=PACK))
        gain_size = keep.tile([P, PACK], F32, name="gain_size")
        gain_sign = keep.tile([P, PACK], F32, name="gain_sign")
        minus_sign = keep.tile([P, PACK], F32, name="minus_sign")
        nc.scalar.activation(gain_size[:], gain[:], ACT.Abs)
        nc.scalar.activation(gain_sign[:], gain[:], ACT.Sign)
        nc.scalar.activation(minus_sign[:], gain[:], ACT.Sign, scale=-1.0)

        w1_grouped = keep.tile([P, PACK, P, PACK], BF16, name="w1_grouped", tag="page0", align_bytes=64)
        nc.vector.tensor_copy(
            w1_grouped[:].rearrange("p t m j -> p m j t"), w1_raw[:].rearrange("p j (m t) -> p m j t", t=PACK)
        )
        w1_codes = keep.tile([P, H], U32, name="w1_codes", tag="page3", align_bytes=64)
        w1_plane = keep.tile([P, H], U8, name="w1_plane", align_bytes=64)
        nc.vector.quantize_mx(
            out=w1_codes[:].bitcast(FP8X4), scales=w1_plane[:], in_=w1_grouped[:].rearrange("p t m j -> p (t m j)")
        )

        x_codes = []
        for c in range(2):
            codes = keep.tile([P, CHUNK], U32, name=f"x_codes{c}", align_bytes=64)
            nc.vector.tensor_copy(codes[:], word_table[:].indirect(entries(offs_sb, c)))
            x_codes.append(codes)
        sized = [keep.tile([P, S], F32, name=f"sized{t}") for t in range(PACK)]

        def first_product(t, c):
            bank = psum.tile([P, CHUNK], F32, name=f"y_bank{t}_{c}", tag=f"bank{2 * t + c}")
            nc.tensor.matmul_mx(
                out=bank[:],
                lhsT=w1_codes[:, t * P : (t + 1) * P].bitcast(FP8X4),
                lhsT_scale=w1_plane[:, t * P : (t + 1) * P],
                rhs=x_codes[c][:].bitcast(FP8X4),
                rhs_scale=x_plane[:, places(c)],
                start=True,
                stop=True,
            )
            if t == 0:
                nc.scalar.activation(sized[t][:, places(c)], bank[:], ACT.Copy, scale=gain_size[:, t : t + 1])
            else:
                nc.vector.tensor_scalar(sized[t][:, places(c)], bank[:], gain_size[:, t : t + 1], None, ALU.mult)

        for c in range(2):
            for t in range(2):
                first_product(t, c)
        for t in range(2, PACK):
            for c in range(2):
                first_product(t, c)

        w2_raw = keep.tile([P, PACK, N], F32, name="w2_raw", tag="weights")
        nc.sync.dma_start(w2_raw[:], w2.rearrange("(p j) c -> p j c", j=PACK))
        mem_rows = mem.rearrange("(b t r) u -> t b r u", t=PACK, r=BLOCK_ROWS)
        out_rows = out.rearrange("(b t r) u -> t b r u", t=PACK, r=BLOCK_ROWS)
        page = []
        for t in range(PACK):
            tile = keep.tile([P, U], F32, name=f"page{t}", tag=f"page{t}", align_bytes=64)
            nc.sync.dma_start(tile[:], mem_rows[t])
            page.append(tile)

        diff = keep.tile([P, PACK, CHUNK], F32, name="diff", tag="diff", align_bytes=64)
        z_rows = keep.tile([P, PACK, CHUNK], BF16, name="z_rows", tag="z_rows", align_bytes=64)

        def fetch_pair(c, t, tag_1, tag_2, on_vector=False):
            at_1 = chunk_tile(f"at_n1_{c}_{t}", tag_1)
            at_2 = chunk_tile(f"at_n2_{c}_{t}", tag_2)
            for dst, list_tile in ((at_1, n1_sb), (at_2, n2_sb)):
                looked_up = sized[t][:].indirect(entries(list_tile, c))
                if on_vector:
                    nc.vector.tensor_copy(dst[:], looked_up)
                else:
                    nc.scalar.activation(dst[:], looked_up, ACT.Copy)
            return at_1, at_2

        def smaller(c, t, pair, tag):
            low = chunk_tile(f"low{c}_{t}", tag)
            nc.vector.tensor_tensor(low[:], pair[0][:], pair[1][:], ALU.min)
            return low

        def subtract_first(t, low):
            nc.vector.tensor_tensor(diff[:, t, :], sized[t][:, places(0)], low[:], ALU.subtract)

        def subtract_second(t, low):
            nc.vector.scalar_tensor_tensor(
                z_rows[:, t, :], low[:], minus_sign[:, t : t + 1], signed[:, t, :], ALU.mult, ALU.add
            )

        def quantise_z(c):
            z = keep.tile([P, CHUNK, PACK], BF16, name=f"z{c}", tag=f"z{c}", align_bytes=64)
            woven = z[:].rearrange("p (n i) t -> p n t i", i=RUN)
            if c == 0:
                nc.vector.tensor_tensor(
                    woven,
                    diff[:].rearrange("p t (n i) -> p n t i", i=RUN),
                    gain_sign[:].unsqueeze(1).unsqueeze(3).to_broadcast([P, CHUNK // RUN, PACK, RUN]),
                    ALU.mult,
                )
            else:
                nc.vector.tensor_copy(woven, z_rows[:].rearrange("p t (n i) -> p n t i", i=RUN))
            z_codes = keep.tile([P, CHUNK], U32, name=f"z_codes{c}", align_bytes=64)
            z_plane = keep.tile([P, CHUNK], U8, name=f"z_plane{c}", align_bytes=64)
            nc.vector.quantize_mx(
                out=z_codes[:].bitcast(FP8X4), scales=z_plane[:], in_=z[:].rearrange("p n t -> p (n t)")
            )
            return z_codes, z_plane

        def quantise_w2(tiles, tag, copy):
            count = len(tiles)
            grouped = keep.tile([P, count, P, PACK], BF16, name=f"w2_grouped{tiles[0]}", tag=tag, align_bytes=64)
            codes = keep.tile([P, count, P], U32, name=f"w2_codes{tiles[0]}", align_bytes=64)
            plane = keep.tile([P, count, P], U8, name=f"w2_plane{tiles[0]}", align_bytes=64)
            halves = BLOCK_ROWS // RUN
            for a, t in enumerate(tiles):
                copy(
                    grouped[:, a].rearrange("p (b s i) j -> p b s j i", s=halves, i=RUN),
                    w2_raw[:].rearrange("p j (b t s i) -> p t b s j i", t=PACK, s=halves, i=RUN)[:, t],
                )
            nc.vector.quantize_mx(
                out=codes[:].rearrange("p a m -> p (a m)").bitcast(FP8X4),
                scales=plane[:].rearrange("p a m -> p (a m)"),
                in_=grouped[:].rearrange("p a m j -> p (a m j)"),
            )
            return [(codes[:, a], plane[:, a]) for a in range(count)]

        def fetch_old(c, t, old_half):
            nc.scalar.activation(old_half, page[t][:].indirect(entries(n3_sb, c)), ACT.Copy, scale=0.5)

        def second_product(t, z_quantised, h):
            nc.tensor.matmul_mx(
                out=h,
                lhsT=w2_quantised[t][0].bitcast(FP8X4),
                lhsT_scale=w2_quantised[t][1],
                rhs=z_quantised[0][:].bitcast(FP8X4),
                rhs_scale=z_quantised[1][:],
                start=True,
                stop=True,
            )

        def tanh_half(th, h):
            nc.scalar.activation(th, h, ACT.Tanh, scale=-0.5)

        def silu(gated, h):
            nc.scalar.activation(gated, h, ACT.Silu)

        def keep_old(kept, old_half, th):
            nc.vector.scalar_tensor_tensor(kept, th, 1.0, old_half, ALU.add, ALU.mult)

        def write_page(c, t, kept, gated):
            nc.vector.tensor_tensor(page[t][:].indirect(entries(n3_sb, c)), kept, gated, ALU.add)

        for t in range(PACK):
            pair = fetch_pair(0, t, f"at_n1_{t}", f"at_n2_{t}", on_vector=t == 1)
            subtract_first(t, smaller(0, t, pair, f"low0_{t}"))
        w2_quantised = quantise_w2([0], "at_n1_2", nc.scalar.copy)
        pair = fetch_pair(1, 0, "at_n1_0", "at_n2_0")
        signed = keep.tile([P, PACK, CHUNK], F32, name="signed", tag="at_n2_3", align_bytes=64)
        for t in range(PACK):
            nc.scalar.activation(signed[:, t, :], sized[t][:, places(1)], ACT.Copy, scale=gain_sign[:, t : t + 1])
        z_first = quantise_z(0)
        subtract_second(0, smaller(1, 0, pair, "z0"))
        w2_quantised.extend(quantise_w2(list(range(1, PACK)), "diff", nc.vector.tensor_copy))

        def ring(t):
            swap = [f"ring_b{t % 2}", f"ring_c{t % 2}"]
            return f"ring_a{t % 2}", swap[t // 2], swap[1 - t // 2]

        h_first, old_first, th_first, gated_first = {}, {}, {}, {}

        def prepare_first(t):
            tag_th, tag_old = ring(t)[:2]
            old_first[t] = chunk_tile(f"old0_{t}", tag_old)
            fetch_old(0, t, old_first[t][:])
            h_first[t] = psum.tile([P, CHUNK], F32, name=f"h_bank0_{t}", tag=f"bank{PACK + t}")
            second_product(t, z_first, h_first[t][:])
            th_first[t] = chunk_tile(f"th0_{t}", tag_th)
            tanh_half(th_first[t][:], h_first[t][:])

        def silu_first(t, tag):
            gated_first[t] = chunk_tile(f"gated0_{t}", tag)
            silu(gated_first[t][:], h_first[t][:])

        def kept_first(t):
            kept = chunk_tile(f"kept0_{t}", f"kept0_{t}")
            keep_old(kept[:], old_first[t][:], th_first[t][:])
            return kept

        prepare_first(0)
        silu_first(0, ring(0)[2])
        prepare_first(1)
        for t in range(LAST):
            kept = kept_first(t)
            pair = fetch_pair(1, t + 1, *ring(t)[:2])
            if t + 1 < LAST:
                silu_first(t + 1, ring(t + 1)[2])
            write_page(0, t, kept[:], gated_first[t][:])
            subtract_second(t + 1, smaller(1, t + 1, pair, f"low1_{t + 1}"))
            if t + 2 < PACK:
                prepare_first(t + 2)
        kept = kept_first(LAST)

        old_second = [keep.tile([P, 2, CHUNK], F32, name="old1_0", tag=ring(2)[0], align_bytes=64)]
        for t in range(2):
            fetch_old(1, t, old_second[0][:, t, :])
        z_second = quantise_z(1)
        silu_first(LAST, "z_rows")
        old_second.append(keep.tile([P, 2, CHUNK], F32, name="old1_1", tag="z1", align_bytes=64))
        fetch_old(1, 2, old_second[1][:, 0, :])
        write_page(0, LAST, kept[:], gated_first[LAST][:])
        for g in range(2):
            h_two = psum.tile([P, 2, CHUNK], F32, name=f"h_bank1_{g}", tag=f"bank{g}")
            th_two = keep.tile([P, 2, CHUNK], F32, name=f"th1_{g}")
            gated_two = keep.tile([P, 2, CHUNK], F32, name=f"gated1_{g}")
            kept_two = keep.tile([P, 2, CHUNK], F32, name=f"kept1_{g}")
            for a in range(2):
                second_product(2 * g + a, z_second, h_two[:, a, :])
            tanh_half(th_two[:], h_two[:])
            silu(gated_two[:], h_two[:])
            if g == 0:
                fetch_old(1, LAST, old_second[1][:, 1, :])
            keep_old(kept_two[:], old_second[g][:], th_two[:])
            for a in range(2):
                t = 2 * g + a
                write_page(1, t, kept_two[:, a, :], gated_two[:, a, :])
                nc.sync.dma_start(out_rows[t], page[t][:])
